import numpy as np
import ml_dtypes


def mxq(x, axis, fmt="e4m3"):
    dtype, down = {"e4m3": (ml_dtypes.float8_e4m3fn, 7), "e5m2": (ml_dtypes.float8_e5m2, 14)}[fmt]
    v = np.moveaxis(np.asarray(x, np.float32).astype(ml_dtypes.bfloat16).astype(np.float64), axis, -1)
    blocks = v.reshape(v.shape[:-1] + (-1, 32))
    amax = np.abs(blocks).max(-1, keepdims=True)
    byte = np.maximum(np.where(amax > 0, np.frexp(amax)[1] - 1 + 127, 0) - down, 1)
    scale = np.exp2(byte - 127.0)
    codes = (blocks / scale).astype(np.float32).astype(dtype).astype(np.float64)
    return np.moveaxis((codes * scale).reshape(v.shape), -1, axis)


WIDE = False


def mx_kscale(k):
    if not WIDE:
        return np.ones(k)
    levels = np.array([10, -10, 5, -5, 0])
    if k % 512:
        return np.exp2(np.random.permutation(np.resize(levels, k // 32))).repeat(32)
    a = np.empty((k // 512, 16))
    for p in range(k // 512):
        a[p, :8] = np.random.permutation(np.resize(levels, 8))
        for g in range(8):
            far = levels[np.abs(levels - a[p, g]) >= 10]
            a[p, g + 8] = far[np.random.randint(len(far))]
    return np.exp2(a.ravel()).repeat(32)


def f64(x):
    return np.asarray(x).astype(np.float64)


def striped(idx):
    return np.tile(idx.reshape(-1, 16).T, (8, 1)).astype(np.uint16)


def unstriped(offs):
    return offs[:16].T.reshape(-1).astype(np.int64)


E2M1 = np.array([0.0, 0.5, 1.0, 1.5, 2.0, 3.0, 4.0, 6.0, -0.0, -0.5, -1.0, -1.5, -2.0, -3.0, -4.0, -6.0])


def pack_weight(w, fmt):
    k, n = w.shape
    w = f64(np.asarray(w, np.float32).astype(ml_dtypes.bfloat16)).reshape(k // 32, 32, n)
    amax = np.abs(w).max(1)
    if fmt == "e4m3":
        byte = np.frexp(amax)[1] - 1 + 127 - 7
    else:
        mant, ex = np.frexp(amax / 6.0)
        byte = np.where(mant > 0.5, ex, ex - 1) + 127
    byte = np.clip(np.where(amax > 0, byte, 1), 1, 254)
    scaled = (w * np.exp2(127.0 - byte)[:, None, :]).reshape(k, n).astype(np.float32)
    by_word = np.ascontiguousarray(scaled.reshape(k // 512, 128, 4, n).transpose(0, 1, 3, 2))
    if fmt == "e4m3":
        words = by_word.astype(ml_dtypes.float8_e4m3fn).view(np.uint8)
    else:
        c = by_word.astype(ml_dtypes.float4_e2m1fn).view(np.uint8) & 0xF
        words = (c[..., 0::2] | (c[..., 1::2] << 4)).reshape(k // 512, 128, 2 * n)
    return np.ascontiguousarray(words), np.ascontiguousarray(byte.astype(np.uint8).reshape(k // 512, 16, n))


def unpack_weight(words, scales, fmt):
    g, _, n = scales.shape
    words = np.ascontiguousarray(words).reshape(g, 128, n, -1)
    if fmt == "e4m3":
        vals = words.view(ml_dtypes.float8_e4m3fn).astype(np.float64)
    else:
        nib = np.empty((g, 128, n, 4), np.uint8)
        nib[..., 0::2] = words & 0xF
        nib[..., 1::2] = words >> 4
        vals = E2M1[nib]
    vals = vals * np.repeat(np.exp2(scales.astype(np.float64) - 127.0), 8, axis=1)[..., None]
    return vals.transpose(0, 1, 3, 2).reshape(g * 512, n)


def gelu(v):
    return 0.5 * v * (1.0 + np.tanh(np.sqrt(2.0 / np.pi) * (v + 0.044715 * v**3)))


def bf(x):
    return np.asarray(x, np.float32).astype(ml_dtypes.bfloat16)


def planes(Y):
    n, m = Y.shape
    b = f64(bf(Y)).reshape(n // 32, 32, m)
    amax = np.abs(b).max(1)
    byte = np.clip(np.where(amax > 0, np.frexp(amax)[1] - 1 + 127 - 7, 1), 1, 254)
    codes = (b * np.exp2(127.0 - byte)[:, None, :]).reshape(n, m).astype(np.float32).astype(ml_dtypes.float8_e4m3fn).view(np.uint8)
    words = codes.reshape(n // 512, 128, 4, m).transpose(0, 1, 3, 2)
    return np.ascontiguousarray(words), np.ascontiguousarray(byte.astype(np.uint8).reshape(n // 512, 16, m))


K, H, N, T, S, T2 = 1024, 1024, 512, 2048, 1024, 2048

def setup_inputs():
    n = np.random.standard_normal
    s = mx_kscale(K)[:, None]
    u = mx_kscale(H)[:, None]
    tab_words, tab_scales = pack_weight(n((K, T)) * s, "e4m3")
    w2_words, w2_scales = pack_weight(n((H, N)) / np.sqrt(H) / u, "e2m1")
    return {
        "tab_words": tab_words, "tab_scales": tab_scales,
        "offs": striped(np.random.permutation(T)[:S]),
        "offs2": striped(np.random.permutation(T2)[:S]),
        "w1": (n((K, H)) / np.sqrt(K) / s * u.T).astype(np.float32),
        "lo": (-(0.6 + 0.3 * np.abs(n(H))) * u[:, 0]).astype(np.float32),
        "hi": ((0.6 + 0.3 * np.abs(n(H))) * u[:, 0]).astype(np.float32),
        "wgs": np.exp(0.3 * n((128, S))).astype(np.float32),
        "page0": (n((H, T2)) * u).astype(np.float32),
        "w2_words": w2_words, "w2_scales": w2_scales,
        "load": n((N, T2)).astype(np.float32),
    }

def reference(tab_words, tab_scales, offs, offs2, w1, lo, hi, wgs, page0, w2_words, w2_scales, load):
    v = unpack_weight(tab_words, tab_scales, "e4m3")[:, unstriped(offs)]
    a = mxq(f64(w1), 0, "e4m3").T @ v
    h = np.minimum(np.maximum(a, f64(lo)[:, None]), f64(hi)[:, None])
    page = f64(page0).copy()
    page[:, unstriped(offs2)] = np.tile(f64(wgs), (H // 128, 1)) * h
    w2 = unpack_weight(w2_words, w2_scales, "e2m1")
    b = w2.T @ mxq(page, 0, "e4m3")
    y = b / (1.0 + np.abs(f64(load)))
    words, scales = planes(page)
    return y, page, words, scales

@@ -1,0 +1,273 @@
+from contextlib import ExitStack
+
+import concourse.mybir as mybir
+
+K, H, N, T, S, T2 = 1024, 1024, 512, 2048, 1024, 2048
+FLOPS = 2 * K * H * S + 2 * H * N * T2
+
+F32 = mybir.dt.float32
+BF16 = mybir.dt.bfloat16
+I32 = mybir.dt.int32
+U32 = mybir.dt.uint32
+U16 = mybir.dt.uint16
+U8 = mybir.dt.uint8
+FP8X4 = mybir.dt.float8_e4m3fn_x4
+FP4X4 = mybir.dt.float4_e2m1fn_x4
+ALU = mybir.AluOpType
+ACT = mybir.ActivationFunctionType
+
+P = 128
+PACK = 4
+PASS = P * PACK
+QUADS = 4
+BANK = 512
+K_PASSES = K // PASS
+GROUPS = H // PASS
+PLANES = GROUPS * PACK
+CHUNKS = T2 // BANK
+N_TILES = N // P
+
+
+def tile_list_elevator_fleet_archive_kernel(
+    tc, tab_words, tab_scales, offs, offs2, w1, lo, hi, wgs, page0, w2_words, w2_scales, load,
+    out_0, out_1, out_2, out_3,
+):
+    nc = tc.nc
+    with ExitStack() as ctx:
+        lists = ctx.enter_context(tc.tile_pool(name="lists", bufs=1))
+        sb = ctx.enter_context(tc.tile_pool(name="sb", bufs=1))
+        psum = ctx.enter_context(tc.psum_pool(name="psum", bufs=8))
+
+        def tile(name, shape, dtype, tag=None, bufs=1):
+            return sb.tile(shape, dtype, name=name, tag=tag or name, bufs=bufs, align_bytes=64)
+
+        idx = lists.tile([P, S // 16], U16, name="idx")
+        idx2 = lists.tile([P, S // 16], U16, name="idx2")
+        tab_w = [tile("tab_w%d" % a, [P, T], I32) for a in range(K_PASSES)]
+        tab_s = tile("tab_s", [P, T], U8)
+        w1_raw = {
+            (g, a): tile("w1_raw%d%d" % (g, a), [P, PACK, PASS], F32, tag="slot%d%d" % (g, a))
+            for g in range(GROUPS) for a in range(K_PASSES)
+        }
+        lo_t = tile("lo_t", [P, GROUPS, PACK], F32)
+        hi_t = tile("hi_t", [P, GROUPS, PACK], F32)
+        wgs_t = [tile("wgs%d" % t, [P, S], F32) for t in range(PACK)]
+        page = [tile("page%d" % k, [P, T2], F32) for k in range(PLANES)]
+        damp = tile("damp", [P, N_TILES, T2], F32)
+        w2_w = tile("w2_w", [P, GROUPS, 2 * N], U8)
+        w2_s = tile("w2_s", [P, GROUPS, N], U8)
+
+        w1_rows = w1.rearrange("(a p j) r -> a p j r", a=K_PASSES, j=PACK)
+        wgs_rows = wgs.rearrange("(q t) j -> t q j", t=PACK)
+        page_rows = page0.rearrange("(g p t) m -> g t p m", g=GROUPS, t=PACK)
+        out1_rows = out_1.rearrange("(g p t) m -> g t p m", g=GROUPS, t=PACK)
+        load_rows = load.rearrange("(b p) m -> p b m", p=P)
+        out0_rows = out_0.rearrange("(b p) m -> p b m", p=P)
+
+        def load_w1(g, a):
+            nc.sync.dma_start(out=w1_raw[g, a][:], in_=w1_rows[a, :, :, g * PASS : (g + 1) * PASS])
+
+        def load_table(a):
+            nc.sync.dma_start(out=tab_w[a][:], in_=tab_words[a].rearrange("p t i -> p (t i)").bitcast(I32))
+
+        def load_wgs(t):
+            for q in (0, 2, 1, 3):
+                nc.sync.dma_start(out=wgs_t[t][32 * q : 32 * q + 32, :], in_=wgs_rows[t])
+
+        def load_page(k):
+            nc.sync.dma_start(out=page[k][:], in_=page_rows[k // PACK, k % PACK])
+
+        def load_load(b):
+            nc.sync.dma_start(out=damp[:, b, :], in_=load_rows[:, b, :])
+
+        nc.vector.memset(tab_s[:].bitcast(I32), 0)
+        nc.vector.memset(w2_s[:].bitcast(I32), 0)
+        for q in range(QUADS):
+            nc.scalar.dma_start(
+                out=tab_s[32 * q : 32 * q + 4 * K_PASSES, :].bitcast(I32),
+                in_=tab_scales[:, 4 * q : 4 * q + 4, :].bitcast(I32),
+            )
+        nc.scalar.dma_start(out=lo_t[:], in_=lo.rearrange("(g p t) -> p g t", g=GROUPS, t=PACK))
+        nc.scalar.dma_start(out=hi_t[:], in_=hi.rearrange("(g p t) -> p g t", g=GROUPS, t=PACK))
+
+        nc.sync.dma_start(idx[:], offs)
+        load_w1(0, 0)
+        load_table(0)
+        load_table(1)
+        load_w1(0, 1)
+        nc.sync.dma_start(idx2[:], offs2)
+        load_wgs(0)
+        load_page(0)
+        load_load(0)
+        load_page(1)
+        load_wgs(1)
+        load_load(1)
+        load_page(2)
+        load_wgs(2)
+        load_w1(1, 0)
+        load_w1(1, 1)
+        load_load(2)
+        load_page(3)
+        load_wgs(3)
+        load_load(3)
+        for k in range(PACK, PLANES):
+            load_page(k)
+        nc.sync.dma_start(out=w2_w[:].bitcast(I32), in_=w2_words.rearrange("g p c -> p g c").bitcast(I32))
+        for q in range(QUADS):
+            nc.sync.dma_start(
+                out=w2_s[32 * q : 32 * q + 4, :, :].bitcast(I32),
+                in_=w2_scales[:, 4 * q : 4 * q + 4, :].rearrange("g r c -> r g c").bitcast(I32),
+            )
+
+        got_s = tile("got_s", [P, S], U8)
+        got_w = [tile("got_w%d" % a, [P, S], I32) for a in range(K_PASSES)]
+        nc.vector.tensor_copy(got_s[:], tab_s[:].indirect(idx[:]))
+        for a in range(K_PASSES):
+            nc.vector.tensor_copy(got_w[a][:].bitcast(U32), tab_w[a][:].bitcast(U32).indirect(idx[:]))
+
+        w1_w, w1_s = {}, {}
+
+        def quantize_w1(g):
+            for a in range(K_PASSES):
+                dealt = tile("w1_bf%d%d" % (g, a), [P, PACK, P, PACK], BF16, tag="w1_bf%d" % a)
+                src = w1_raw[g, a][:].rearrange("p j (m t) -> p m t j", t=PACK)
+                dst = dealt[:].rearrange("p t m j -> p m t j")
+                if (g, a) == (0, 1):
+                    nc.vector.tensor_copy(out=dst, in_=src)
+                else:
+                    nc.scalar.copy(out=dst, in_=src)
+                w1_w[g, a] = tile("w1_w%d%d" % (g, a), [P, PASS], I32)
+                w1_s[g, a] = tile("w1_s%d%d" % (g, a), [P, PASS], U8)
+                flat = dealt[:].rearrange("p t m j -> p (t m j)")
+                cuts = (0, 128, 256, 512) if (g, a) == (0, 1) else (0, 512)
+                for c0, c1 in zip(cuts, cuts[1:]):
+                    nc.vector.quantize_mx(
+                        out=w1_w[g, a][:, c0:c1].bitcast(FP8X4),
+                        scales=w1_s[g, a][:, c0:c1],
+                        in_=flat[:, PACK * c0 : PACK * c1],
+                    )
+
+        half = T2 // 2
+        pair_tags = ("slot00", "slot01", "pairs2", "pairs3")
+
+        def damping(b):
+            parts = [damp[:, b, i * half : (i + 1) * half] for i in range(2)]
+            work = [tile("work%d%d" % (b, i), [P, half], F32, tag=pair_tags[(2 * b + i) % CHUNKS]) for i in range(2)]
+            for i in range(2):
+                nc.scalar.activation(out=work[i][:], in_=parts[i], func=ACT.Abs)
+            for i in range(2):
+                nc.scalar.activation(out=work[i][:], in_=work[i][:], func=ACT.Abs_reciprocal_sqrt, bias=1.0)
+            for i in range(2):
+                nc.scalar.activation(out=parts[i], in_=work[i][:], func=ACT.Square)
+
+        quantize_w1(0)
+        damping(0)
+        damping(1)
+        quantize_w1(1)
+        damping(2)
+        damping(3)
+
+        clipped = {}
+
+        def first_product(k):
+            g, t = divmod(k, PACK)
+            if k == PLANES - 1:
+                clipped[k] = tile("h_last", [P, S], F32, tag="slot11")
+            elif k == PACK - 1:
+                clipped[k] = tile("h_mid", [P, S], F32, tag="w1_bf1")
+            else:
+                clipped[k] = tile("h%d" % k, [P, S], F32, tag="h", bufs=2)
+            for j0 in range(0, S, BANK):
+                acc = psum.tile([P, BANK], F32, name="acc", tag="bank")
+                for a in range(K_PASSES):
+                    nc.tensor.matmul_mx(
+                        out=acc[:],
+                        lhsT=w1_w[g, a][:, t * P : (t + 1) * P].bitcast(FP8X4),
+                        lhsT_scale=w1_s[g, a][:, t * P : (t + 1) * P],
+                        rhs=got_w[a][:, j0 : j0 + BANK].bitcast(FP8X4),
+                        rhs_scale=got_s[4 * a : P, j0 : j0 + BANK],
+                        start=(a == 0),
+                        stop=(a == K_PASSES - 1),
+                    )
+                nc.vector.tensor_scalar(
+                    out=clipped[k][:, j0 : j0 + BANK], in0=acc[:],
+                    scalar1=lo_t[:, g, t : t + 1], scalar2=hi_t[:, g, t : t + 1],
+                    op0=ALU.max, op1=ALU.min,
+                )
+
+        def scatter(k):
+            nc.vector.tensor_tensor(page[k][:].indirect(idx2[:]), clipped[k][:], wgs_t[k % PACK][:], ALU.mult)
+            nc.sync.dma_start(out=out1_rows[k // PACK, k % PACK], in_=page[k][:])
+
+        page_w = [tile("page_w%d" % g, [P, T2], I32) for g in range(GROUPS)]
+        page_s = [tile("page_s%d" % g, [P, T2], U8) for g in range(GROUPS)]
+        pairs = {}
+
+        def round_plane(k, c):
+            g, t = divmod(k, PACK)
+            if t == 0:
+                pairs[g, c] = tile("pairs%d%d" % (g, c), [P, 2, BANK, 2], BF16, tag=pair_tags[c])
+            nc.scalar.copy(out=pairs[g, c][:, t // 2, :, t % 2], in_=page[k][:, c * BANK : (c + 1) * BANK])
+
+        def quantize_chunk(g, c):
+            cols = slice(c * BANK, (c + 1) * BANK)
+            woven = tile("woven%d%d" % (g, c), [P, BANK * PACK], BF16, tag="slot1%d" % (c % 2))
+            nc.scalar.copy(
+                out=woven[:].bitcast(F32).rearrange("p (m u) -> p m u", u=2),
+                in_=pairs[g, c][:].rearrange("p u m e -> p u (m e)").bitcast(F32).rearrange("p u m -> p m u"),
+            )
+            nc.vector.quantize_mx(out=page_w[g][:, cols].bitcast(FP8X4), scales=page_s[g][:, cols], in_=woven[:])
+
+        def store_words(g, c0, c1):
+            nc.sync.dma_start(
+                out=out_2[g].rearrange("p m t -> p (m t)").bitcast(I32)[:, c0:c1], in_=page_w[g][:, c0:c1]
+            )
+
+        def store_scales(g, queue):
+            for q in range(QUADS):
+                queue.dma_start(
+                    out=out_3[g, 4 * q : 4 * q + 4, :].bitcast(I32),
+                    in_=page_s[g][32 * q : 32 * q + 4, :].bitcast(I32),
+                )
+
+        first_product(0)
+        for k in range(PLANES):
+            if k + 1 < PLANES:
+                first_product(k + 1)
+            scatter(k)
+            if k == PACK - 1:
+                for plane in range(PACK):
+                    for c in range(CHUNKS):
+                        round_plane(plane, c)
+                for c in range(CHUNKS):
+                    quantize_chunk(0, c)
+            if k == PLANES - 2:
+                store_words(0, 0, T2)
+                store_scales(0, nc.sync)
+        for plane in range(PACK, PLANES - 1):
+            for c in range(CHUNKS):
+                round_plane(plane, c)
+        for c in range(CHUNKS):
+            round_plane(PLANES - 1, c)
+            quantize_chunk(1, c)
+            if c % 2 == 1:
+                store_words(1, (c - 1) * BANK, (c + 1) * BANK)
+
+        for c in range(CHUNKS):
+            cols = slice(c * BANK, (c + 1) * BANK)
+            for b in range(N_TILES):
+                acc = psum.tile([P, BANK], F32, name="acc", tag="bank")
+                for g in range(GROUPS):
+                    nc.tensor.matmul_mx(
+                        out=acc[:],
+                        lhsT=w2_w[:, g, 2 * b * P : 2 * (b + 1) * P].bitcast(FP4X4),
+                        lhsT_scale=w2_s[:, g, b * P : (b + 1) * P],
+                        rhs=page_w[g][:, cols].bitcast(FP8X4),
+                        rhs_scale=page_s[g][:, cols],
+                        start=(g == 0),
+                        stop=(g == GROUPS - 1),
+                    )
+                nc.vector.tensor_tensor(damp[:, b, cols], acc[:], damp[:, b, cols], ALU.mult)
+                if b % 2 == 1:
+                    nc.sync.dma_start(out=out0_rows[:, b - 1 : b + 1, cols], in_=damp[:, b - 1 : b + 1, cols])
+        store_scales(1, nc.scalar)

@@ -70,9 +70,9 @@ def tile_list_elevator_fleet_archive_kernel(
         def load_table(a):
             nc.sync.dma_start(out=tab_w[a][:], in_=tab_words[a].rearrange("p t i -> p (t i)").bitcast(I32))
 
-        def load_wgs(t):
+        def load_wgs(t, j0=0, j1=S):
             for q in (0, 2, 1, 3):
-                nc.sync.dma_start(out=wgs_t[t][32 * q : 32 * q + 32, :], in_=wgs_rows[t])
+                nc.sync.dma_start(out=wgs_t[t][32 * q : 32 * q + 32, j0:j1], in_=wgs_rows[t, :, j0:j1])
 
         def load_page(k):
             nc.sync.dma_start(out=page[k][:], in_=page_rows[k // PACK, k % PACK])
@@ -91,13 +91,14 @@ def tile_list_elevator_fleet_archive_kernel(
         nc.scalar.dma_start(out=hi_t[:], in_=hi.rearrange("(g p t) -> p g t", g=GROUPS, t=PACK))
 
         nc.sync.dma_start(idx[:], offs)
-        load_w1(0, 0)
         load_table(0)
-        load_table(1)
+        load_w1(0, 0)
         load_w1(0, 1)
+        load_table(1)
         nc.sync.dma_start(idx2[:], offs2)
-        load_wgs(0)
+        load_wgs(0, 0, BANK)
         load_page(0)
+        load_wgs(0, BANK, S)
         load_load(0)
         load_page(1)
         load_wgs(1)
@@ -105,10 +106,10 @@ def tile_list_elevator_fleet_archive_kernel(
         load_page(2)
         load_wgs(2)
         load_w1(1, 0)
-        load_w1(1, 1)
         load_load(2)
         load_page(3)
         load_wgs(3)
+        load_w1(1, 1)
         load_load(3)
         for k in range(PACK, PLANES):
             load_page(k)
@@ -119,84 +120,127 @@ def tile_list_elevator_fleet_archive_kernel(
                 in_=w2_scales[:, 4 * q : 4 * q + 4, :].rearrange("g r c -> r g c").bitcast(I32),
             )
 
+        warm = tile("warm", [P, 1], F32)
+        nc.scalar.activation(out=warm[:], in_=lo_t[:, 0, 0:1], func=ACT.Abs_reciprocal_sqrt)
+
         got_s = tile("got_s", [P, S], U8)
         got_w = [tile("got_w%d" % a, [P, S], I32) for a in range(K_PASSES)]
-        nc.vector.tensor_copy(got_s[:], tab_s[:].indirect(idx[:]))
-        for a in range(K_PASSES):
-            nc.vector.tensor_copy(got_w[a][:].bitcast(U32), tab_w[a][:].bitcast(U32).indirect(idx[:]))
+
+        def gather_words(a, j0, j1):
+            window = tab_w[a][:].bitcast(U32)
+            nc.vector.tensor_copy(got_w[a][:, j0:j1].bitcast(U32), window.indirect(idx[:, j0 // 16 : j1 // 16]))
 
         w1_w, w1_s = {}, {}
 
-        def quantize_w1(g):
-            for a in range(K_PASSES):
-                dealt = tile("w1_bf%d%d" % (g, a), [P, PACK, P, PACK], BF16, tag="w1_bf%d" % a)
-                src = w1_raw[g, a][:].rearrange("p j (m t) -> p m t j", t=PACK)
-                dst = dealt[:].rearrange("p t m j -> p m t j")
-                if (g, a) == (0, 1):
-                    nc.vector.tensor_copy(out=dst, in_=src)
-                else:
-                    nc.scalar.copy(out=dst, in_=src)
-                w1_w[g, a] = tile("w1_w%d%d" % (g, a), [P, PASS], I32)
-                w1_s[g, a] = tile("w1_s%d%d" % (g, a), [P, PASS], U8)
-                flat = dealt[:].rearrange("p t m j -> p (t m j)")
-                cuts = (0, 128, 256, 512) if (g, a) == (0, 1) else (0, 512)
-                for c0, c1 in zip(cuts, cuts[1:]):
-                    nc.vector.quantize_mx(
-                        out=w1_w[g, a][:, c0:c1].bitcast(FP8X4),
-                        scales=w1_s[g, a][:, c0:c1],
-                        in_=flat[:, PACK * c0 : PACK * c1],
-                    )
+        def quantize_w1(g, a, vector_share, cuts):
+            dealt = tile("w1_bf%d%d" % (g, a), [P, PACK, P, PACK], BF16, tag="w1_bf%d" % a)
+            src = w1_raw[g, a][:].rearrange("p j (m t) -> p m t j", t=PACK)
+            dst = dealt[:].rearrange("p t m j -> p m t j")
+            if vector_share > 0:
+                nc.vector.tensor_copy(out=dst[:, :vector_share], in_=src[:, :vector_share])
+            if vector_share < P:
+                nc.scalar.copy(out=dst[:, vector_share:], in_=src[:, vector_share:])
+            w1_w[g, a] = tile("w1_w%d%d" % (g, a), [P, PASS], I32)
+            w1_s[g, a] = tile("w1_s%d%d" % (g, a), [P, PASS], U8)
+            flat = dealt[:].rearrange("p t m j -> p (t m j)")
+            for c0, c1 in zip(cuts, cuts[1:]):
+                nc.vector.quantize_mx(
+                    out=w1_w[g, a][:, c0:c1].bitcast(FP8X4),
+                    scales=w1_s[g, a][:, c0:c1],
+                    in_=flat[:, PACK * c0 : PACK * c1],
+                )
 
-        half = T2 // 2
-        pair_tags = ("slot00", "slot01", "pairs2", "pairs3")
+        pair_tags = ("slot11", "work0", "work1", "work2")
+        last = slice((CHUNKS - 1) * BANK, T2)
 
         def damping(b):
-            parts = [damp[:, b, i * half : (i + 1) * half] for i in range(2)]
-            work = [tile("work%d%d" % (b, i), [P, half], F32, tag=pair_tags[(2 * b + i) % CHUNKS]) for i in range(2)]
-            for i in range(2):
-                nc.scalar.activation(out=work[i][:], in_=parts[i], func=ACT.Abs)
-            for i in range(2):
-                nc.scalar.activation(out=work[i][:], in_=work[i][:], func=ACT.Abs_reciprocal_sqrt, bias=1.0)
-            for i in range(2):
-                nc.scalar.activation(out=parts[i], in_=work[i][:], func=ACT.Square)
+            nc.scalar.activation(out=damp[:, b, :], in_=damp[:, b, :], func=ACT.Abs)
+            work = [tile("root%d%d" % (b, c), [P, BANK], F32, tag=pair_tags[c + 1]) for c in range(CHUNKS - 1)]
+            for c in range(CHUNKS - 1):
+                nc.scalar.activation(
+                    out=work[c][:], in_=damp[:, b, c * BANK : (c + 1) * BANK], func=ACT.Abs_reciprocal_sqrt, bias=1.0
+                )
+            nc.scalar.activation(out=damp[:, b, last], in_=damp[:, b, last], func=ACT.Abs_reciprocal_sqrt, bias=1.0)
+            for c in range(CHUNKS - 1):
+                nc.scalar.activation(out=damp[:, b, c * BANK : (c + 1) * BANK], in_=work[c][:], func=ACT.Square)
 
-        quantize_w1(0)
-        damping(0)
-        damping(1)
-        quantize_w1(1)
-        damping(2)
-        damping(3)
+        nc.vector.tensor_copy(got_s[:], tab_s[:].indirect(idx[:]))
+        gather_words(0, 0, S)
+        quantize_w1(0, 0, 0, (0, PASS))
+        quantize_w1(0, 1, P, (0, PASS))
+        gather_words(1, 0, BANK)
+        gather_words(1, BANK, S)
 
         clipped = {}
 
-        def first_product(k):
+        def clip(k, out, in0):
             g, t = divmod(k, PACK)
+            nc.vector.tensor_scalar(
+                out=out, in0=in0, scalar1=lo_t[:, g, t : t + 1], scalar2=hi_t[:, g, t : t + 1],
+                op0=ALU.max, op1=ALU.min,
+            )
+
+        def clipped_tile(k):
             if k == PLANES - 1:
-                clipped[k] = tile("h_last", [P, S], F32, tag="slot11")
-            elif k == PACK - 1:
-                clipped[k] = tile("h_mid", [P, S], F32, tag="w1_bf1")
-            else:
-                clipped[k] = tile("h%d" % k, [P, S], F32, tag="h", bufs=2)
-            for j0 in range(0, S, BANK):
-                acc = psum.tile([P, BANK], F32, name="acc", tag="bank")
-                for a in range(K_PASSES):
-                    nc.tensor.matmul_mx(
-                        out=acc[:],
-                        lhsT=w1_w[g, a][:, t * P : (t + 1) * P].bitcast(FP8X4),
-                        lhsT_scale=w1_s[g, a][:, t * P : (t + 1) * P],
-                        rhs=got_w[a][:, j0 : j0 + BANK].bitcast(FP8X4),
-                        rhs_scale=got_s[4 * a : P, j0 : j0 + BANK],
-                        start=(a == 0),
-                        stop=(a == K_PASSES - 1),
-                    )
-                nc.vector.tensor_scalar(
-                    out=clipped[k][:, j0 : j0 + BANK], in0=acc[:],
-                    scalar1=lo_t[:, g, t : t + 1], scalar2=hi_t[:, g, t : t + 1],
-                    op0=ALU.max, op1=ALU.min,
+                return tile("h_last", [P, S], F32, tag="slot01")
+            return tile("h%d" % k, [P, S], F32, tag="h%d" % ((k + 1) % 2))
+
+        def product(k, j0):
+            g, t = divmod(k, PACK)
+            acc = psum.tile([P, BANK], F32, name="acc", tag="bank")
+            for a in range(K_PASSES):
+                nc.tensor.matmul_mx(
+                    out=acc[:],
+                    lhsT=w1_w[g, a][:, t * P : (t + 1) * P].bitcast(FP8X4),
+                    lhsT_scale=w1_s[g, a][:, t * P : (t + 1) * P],
+                    rhs=got_w[a][:, j0 : j0 + BANK].bitcast(FP8X4),
+                    rhs_scale=got_s[4 * a : P, j0 : j0 + BANK],
+                    start=(a == 0),
+                    stop=(a == K_PASSES - 1),
                 )
+            return acc
+
+        def first_product(k):
+            if k in sums:
+                clipped[k] = clipped_tile(k)
+                clip(k, clipped[k][:], sums[k])
+                return
+            clipped[k] = clipped_tile(k)
+            for j0 in range(0, S, BANK):
+                clip(k, clipped[k][:, j0 : j0 + BANK], product(k, j0)[:])
+
+        sums = {}
+        first = []
+        for i, j0 in enumerate(range(0, S, BANK)):
+            first.append(tile("h_first%d" % i, [P, BANK], F32, tag="h%d" % i))
+            clip(0, first[i][:], product(0, j0)[:])
+
+        def copy_sums(k, held):
+            sums[k] = held
+            for j0 in range(0, S, BANK):
+                nc.scalar.copy(out=sums[k][:, j0 : j0 + BANK], in_=product(k, j0)[:])
+
+        for k, tag in ((1, "sums1"), (2, "slot00"), (3, "slot01")):
+            copy_sums(k, tile("sums%d" % k, [P, S], F32, tag=tag)[:])
+
+        damping(0)
+        damping(1)
+        quantize_w1(1, 0, 0, (0, PASS))
+        damping(2)
+        quantize_w1(1, 1, 0, (0, P, 2 * P, PASS))
+        damping(3)
+
+        def scatter_first(i):
+            places = idx2[:, i * BANK // 16 : (i + 1) * BANK // 16]
+            nc.vector.tensor_tensor(
+                page[0][:].indirect(places), first[i][:], wgs_t[0][:, i * BANK : (i + 1) * BANK], ALU.mult
+            )
 
         def scatter(k):
-            nc.vector.tensor_tensor(page[k][:].indirect(idx2[:]), clipped[k][:], wgs_t[k % PACK][:], ALU.mult)
+            if k == 0:
+                scatter_first(1)
+            else:
+                nc.vector.tensor_tensor(page[k][:].indirect(idx2[:]), clipped[k][:], wgs_t[k % PACK][:], ALU.mult)
             nc.sync.dma_start(out=out1_rows[k // PACK, k % PACK], in_=page[k][:])
 
         page_w = [tile("page_w%d" % g, [P, T2], I32) for g in range(GROUPS)]
@@ -211,8 +255,9 @@ def tile_list_elevator_fleet_archive_kernel(
 
         def quantize_chunk(g, c):
             cols = slice(c * BANK, (c + 1) * BANK)
-            woven = tile("woven%d%d" % (g, c), [P, BANK * PACK], BF16, tag="slot1%d" % (c % 2))
-            nc.scalar.copy(
+            woven = tile("woven%d%d" % (g, c), [P, BANK * PACK], BF16, tag="slot0%d" % (c % 2))
+            copy = nc.vector.tensor_copy if g == GROUPS - 1 and c < 2 else nc.scalar.copy
+            copy(
                 out=woven[:].bitcast(F32).rearrange("p (m u) -> p m u", u=2),
                 in_=pairs[g, c][:].rearrange("p u m e -> p u (m e)").bitcast(F32).rearrange("p u m -> p m u"),
             )
@@ -230,12 +275,16 @@ def tile_list_elevator_fleet_archive_kernel(
                     in_=page_s[g][32 * q : 32 * q + 4, :].bitcast(I32),
                 )
 
-        first_product(0)
+        scatter_first(0)
         for k in range(PLANES):
             if k + 1 < PLANES:
                 first_product(k + 1)
             scatter(k)
             if k == PACK - 1:
+                copy_sums(5, tile("sums5", [P, S], F32, tag="sums1")[:])
+                last_two = tile("sums67", [P, 2, S], F32, tag="slot10")
+                copy_sums(6, last_two[:, 0, :])
+                copy_sums(7, last_two[:, 1, :])
                 for plane in range(PACK):
                     for c in range(CHUNKS):
                         round_plane(plane, c)
@@ -247,13 +296,8 @@ def tile_list_elevator_fleet_archive_kernel(
         for plane in range(PACK, PLANES - 1):
             for c in range(CHUNKS):
                 round_plane(plane, c)
-        for c in range(CHUNKS):
-            round_plane(PLANES - 1, c)
-            quantize_chunk(1, c)
-            if c % 2 == 1:
-                store_words(1, (c - 1) * BANK, (c + 1) * BANK)
 
-        for c in range(CHUNKS):
+        def second_product(c, factor):
             cols = slice(c * BANK, (c + 1) * BANK)
             for b in range(N_TILES):
                 acc = psum.tile([P, BANK], F32, name="acc", tag="bank")
@@ -267,7 +311,17 @@ def tile_list_elevator_fleet_archive_kernel(
                         start=(g == 0),
                         stop=(g == GROUPS - 1),
                     )
-                nc.vector.tensor_tensor(damp[:, b, cols], acc[:], damp[:, b, cols], ALU.mult)
+                nc.vector.tensor_tensor(factor[:, b, :], acc[:], factor[:, b, :], ALU.mult)
                 if b % 2 == 1:
-                    nc.sync.dma_start(out=out0_rows[:, b - 1 : b + 1, cols], in_=damp[:, b - 1 : b + 1, cols])
-        store_scales(1, nc.scalar)
+                    nc.sync.dma_start(out=out0_rows[:, b - 1 : b + 1, cols], in_=factor[:, b - 1 : b + 1, :])
+
+        for c in range(CHUNKS):
+            round_plane(PLANES - 1, c)
+            quantize_chunk(1, c)
+            store_words(1, c * BANK, (c + 1) * BANK)
+            if c > 0:
+                second_product(c - 1, damp[:, :, (c - 1) * BANK : c * BANK])
+        damp_last = tile("damp_last", [P, N_TILES, BANK], F32, tag="slot11")
+        nc.scalar.activation(out=damp_last[:], in_=damp[:, :, last], func=ACT.Square)
+        store_scales(1, nc.sync)
+        second_product(CHUNKS - 1, damp_last[:])

@@ -20,12 +20,18 @@ P = 128
 PACK = 4
 PASS = P * PACK
 QUADS = 4
+QUAD = P // QUADS
+SCALE_ROWS = 4
+STRIPE = 16
 BANK = 512
+BANKS = 8
 K_PASSES = K // PASS
 GROUPS = H // PASS
 PLANES = GROUPS * PACK
 CHUNKS = T2 // BANK
 N_TILES = N // P
+LEAD = 64
+WOVEN_BY_VECTOR = ((0, 2), (0, 3), (1, 0), (1, 1))
 
 
 def tile_list_elevator_fleet_archive_kernel(
@@ -36,17 +42,17 @@ def tile_list_elevator_fleet_archive_kernel(
     with ExitStack() as ctx:
         lists = ctx.enter_context(tc.tile_pool(name="lists", bufs=1))
         sb = ctx.enter_context(tc.tile_pool(name="sb", bufs=1))
-        psum = ctx.enter_context(tc.psum_pool(name="psum", bufs=8))
+        psum = ctx.enter_context(tc.psum_pool(name="psum", bufs=BANKS))
 
-        def tile(name, shape, dtype, tag=None, bufs=1):
-            return sb.tile(shape, dtype, name=name, tag=tag or name, bufs=bufs, align_bytes=64)
+        def tile(name, shape, dtype, tag=None):
+            return sb.tile(shape, dtype, name=name, tag=tag or name, bufs=1, align_bytes=64)
 
-        idx = lists.tile([P, S // 16], U16, name="idx")
-        idx2 = lists.tile([P, S // 16], U16, name="idx2")
+        idx = lists.tile([P, S // STRIPE], U16, name="idx")
+        idx2 = lists.tile([P, S // STRIPE], U16, name="idx2")
         tab_w = [tile("tab_w%d" % a, [P, T], I32) for a in range(K_PASSES)]
         tab_s = tile("tab_s", [P, T], U8)
         w1_raw = {
-            (g, a): tile("w1_raw%d%d" % (g, a), [P, PACK, PASS], F32, tag="slot%d%d" % (g, a))
+            (g, a): tile("w1_raw%d%d" % (g, a), [P, PACK, PASS], F32, tag="w1_%d%d" % (g, a))
             for g in range(GROUPS) for a in range(K_PASSES)
         }
         lo_t = tile("lo_t", [P, GROUPS, PACK], F32)
@@ -57,7 +63,7 @@ def tile_list_elevator_fleet_archive_kernel(
         w2_w = tile("w2_w", [P, GROUPS, 2 * N], U8)
         w2_s = tile("w2_s", [P, GROUPS, N], U8)
 
-        w1_rows = w1.rearrange("(a p j) r -> a p j r", a=K_PASSES, j=PACK)
+        w1_rows = w1.rearrange("(a p i) r -> a p i r", a=K_PASSES, i=PACK)
         wgs_rows = wgs.rearrange("(q t) j -> t q j", t=PACK)
         page_rows = page0.rearrange("(g p t) m -> g t p m", g=GROUPS, t=PACK)
         out1_rows = out_1.rearrange("(g p t) m -> g t p m", g=GROUPS, t=PACK)
@@ -72,21 +78,22 @@ def tile_list_elevator_fleet_archive_kernel(
 
         def load_wgs(t, j0=0, j1=S):
             for q in (0, 2, 1, 3):
-                nc.sync.dma_start(out=wgs_t[t][32 * q : 32 * q + 32, j0:j1], in_=wgs_rows[t, :, j0:j1])
+                nc.sync.dma_start(out=wgs_t[t][QUAD * q : QUAD * (q + 1), j0:j1], in_=wgs_rows[t, :, j0:j1])
 
         def load_page(k):
             nc.sync.dma_start(out=page[k][:], in_=page_rows[k // PACK, k % PACK])
 
-        def load_load(b):
-            nc.sync.dma_start(out=damp[:, b, :], in_=load_rows[:, b, :])
+        def load_load(b, m0=0):
+            nc.sync.dma_start(out=damp[:, b, m0:], in_=load_rows[:, b, m0:])
 
         nc.vector.memset(tab_s[:].bitcast(I32), 0)
         nc.vector.memset(w2_s[:].bitcast(I32), 0)
         for q in range(QUADS):
             nc.scalar.dma_start(
-                out=tab_s[32 * q : 32 * q + 4 * K_PASSES, :].bitcast(I32),
-                in_=tab_scales[:, 4 * q : 4 * q + 4, :].bitcast(I32),
+                out=tab_s[QUAD * q : QUAD * q + SCALE_ROWS * K_PASSES, :].bitcast(I32),
+                in_=tab_scales[:, SCALE_ROWS * q : SCALE_ROWS * (q + 1), :].bitcast(I32),
             )
+        nc.scalar.dma_start(out=damp[:, 0, :LEAD], in_=load_rows[:, 0, :LEAD])
         nc.scalar.dma_start(out=lo_t[:], in_=lo.rearrange("(g p t) -> p g t", g=GROUPS, t=PACK))
         nc.scalar.dma_start(out=hi_t[:], in_=hi.rearrange("(g p t) -> p g t", g=GROUPS, t=PACK))
 
@@ -99,93 +106,86 @@ def tile_list_elevator_fleet_archive_kernel(
         load_wgs(0, 0, BANK)
         load_page(0)
         load_wgs(0, BANK, S)
-        load_load(0)
+        load_load(0, LEAD)
         load_page(1)
         load_wgs(1)
         load_load(1)
         load_page(2)
         load_wgs(2)
         load_w1(1, 0)
+        load_w1(1, 1)
         load_load(2)
         load_page(3)
         load_wgs(3)
-        load_w1(1, 1)
         load_load(3)
         for k in range(PACK, PLANES):
             load_page(k)
         nc.sync.dma_start(out=w2_w[:].bitcast(I32), in_=w2_words.rearrange("g p c -> p g c").bitcast(I32))
         for q in range(QUADS):
             nc.sync.dma_start(
-                out=w2_s[32 * q : 32 * q + 4, :, :].bitcast(I32),
-                in_=w2_scales[:, 4 * q : 4 * q + 4, :].rearrange("g r c -> r g c").bitcast(I32),
+                out=w2_s[QUAD * q : QUAD * q + SCALE_ROWS, :, :].bitcast(I32),
+                in_=w2_scales[:, SCALE_ROWS * q : SCALE_ROWS * (q + 1), :].rearrange("g r c -> r g c").bitcast(I32),
             )
-
-        warm = tile("warm", [P, 1], F32)
-        nc.scalar.activation(out=warm[:], in_=lo_t[:, 0, 0:1], func=ACT.Abs_reciprocal_sqrt)
 
         got_s = tile("got_s", [P, S], U8)
         got_w = [tile("got_w%d" % a, [P, S], I32) for a in range(K_PASSES)]
 
         def gather_words(a, j0, j1):
             window = tab_w[a][:].bitcast(U32)
-            nc.vector.tensor_copy(got_w[a][:, j0:j1].bitcast(U32), window.indirect(idx[:, j0 // 16 : j1 // 16]))
+            entries = idx[:, j0 // STRIPE : j1 // STRIPE]
+            nc.vector.tensor_copy(got_w[a][:, j0:j1].bitcast(U32), window.indirect(entries))
 
         w1_w, w1_s = {}, {}
 
-        def quantize_w1(g, a, vector_share, cuts):
+        def quantize_w1(g, a, copy):
             dealt = tile("w1_bf%d%d" % (g, a), [P, PACK, P, PACK], BF16, tag="w1_bf%d" % a)
-            src = w1_raw[g, a][:].rearrange("p j (m t) -> p m t j", t=PACK)
-            dst = dealt[:].rearrange("p t m j -> p m t j")
-            if vector_share > 0:
-                nc.vector.tensor_copy(out=dst[:, :vector_share], in_=src[:, :vector_share])
-            if vector_share < P:
-                nc.scalar.copy(out=dst[:, vector_share:], in_=src[:, vector_share:])
+            copy(
+                out=dealt[:].rearrange("p t m i -> p m t i"),
+                in_=w1_raw[g, a][:].rearrange("p i (m t) -> p m t i", t=PACK),
+            )
             w1_w[g, a] = tile("w1_w%d%d" % (g, a), [P, PASS], I32)
             w1_s[g, a] = tile("w1_s%d%d" % (g, a), [P, PASS], U8)
-            flat = dealt[:].rearrange("p t m j -> p (t m j)")
-            for c0, c1 in zip(cuts, cuts[1:]):
-                nc.vector.quantize_mx(
-                    out=w1_w[g, a][:, c0:c1].bitcast(FP8X4),
-                    scales=w1_s[g, a][:, c0:c1],
-                    in_=flat[:, PACK * c0 : PACK * c1],
-                )
+            nc.vector.quantize_mx(
+                out=w1_w[g, a][:].bitcast(FP8X4),
+                scales=w1_s[g, a][:],
+                in_=dealt[:].rearrange("p t m i -> p (t m i)"),
+            )
 
-        pair_tags = ("slot11", "work0", "work1", "work2")
-        last = slice((CHUNKS - 1) * BANK, T2)
+        chunk = [slice(c * BANK, (c + 1) * BANK) for c in range(CHUNKS)]
+        pair_tags = ("w1_11", "work0", "work1", "work2")
 
-        def damping(b):
-            nc.scalar.activation(out=damp[:, b, :], in_=damp[:, b, :], func=ACT.Abs)
-            work = [tile("root%d%d" % (b, c), [P, BANK], F32, tag=pair_tags[c + 1]) for c in range(CHUNKS - 1)]
-            for c in range(CHUNKS - 1):
-                nc.scalar.activation(
-                    out=work[c][:], in_=damp[:, b, c * BANK : (c + 1) * BANK], func=ACT.Abs_reciprocal_sqrt, bias=1.0
-                )
-            nc.scalar.activation(out=damp[:, b, last], in_=damp[:, b, last], func=ACT.Abs_reciprocal_sqrt, bias=1.0)
-            for c in range(CHUNKS - 1):
-                nc.scalar.activation(out=damp[:, b, c * BANK : (c + 1) * BANK], in_=work[c][:], func=ACT.Square)
+        def magnitude(out, in_):
+            nc.scalar.activation(out=out, in_=in_, func=ACT.Abs)
+
+        def root(out, in_):
+            nc.scalar.activation(out=out, in_=in_, func=ACT.Abs_reciprocal_sqrt, bias=1.0)
+
+        def square(out, in_):
+            nc.scalar.activation(out=out, in_=in_, func=ACT.Square)
+
+        def begin_factor(b, m0=0):
+            work = [tile("work%d%d" % (b, c), [P, BANK], F32, tag=pair_tags[c + 1]) for c in range(CHUNKS - 1)]
+            row = damp[:, b, :]
+            magnitude(row[:, m0 : 2 * BANK], row[:, m0 : 2 * BANK])
+            magnitude(work[2][:], row[:, chunk[2]])
+            magnitude(row[:, chunk[3]], row[:, chunk[3]])
+            root(work[0][:, m0:], row[:, m0:BANK])
+            root(work[1][:], row[:, chunk[1]])
+            root(row[:, chunk[2]], work[2][:])
+            square(row[:, m0:BANK], work[0][:, m0:])
+            square(row[:, chunk[1]], work[1][:])
+
+        for step in (magnitude, root, square):
+            step(damp[:, 0, :LEAD], damp[:, 0, :LEAD])
 
         nc.vector.tensor_copy(got_s[:], tab_s[:].indirect(idx[:]))
         gather_words(0, 0, S)
-        quantize_w1(0, 0, 0, (0, PASS))
-        quantize_w1(0, 1, P, (0, PASS))
+        quantize_w1(0, 0, nc.scalar.copy)
+        quantize_w1(0, 1, nc.vector.tensor_copy)
         gather_words(1, 0, BANK)
         gather_words(1, BANK, S)
 
-        clipped = {}
-
-        def clip(k, out, in0):
-            g, t = divmod(k, PACK)
-            nc.vector.tensor_scalar(
-                out=out, in0=in0, scalar1=lo_t[:, g, t : t + 1], scalar2=hi_t[:, g, t : t + 1],
-                op0=ALU.max, op1=ALU.min,
-            )
-
-        def clipped_tile(k):
-            if k == PLANES - 1:
-                return tile("h_last", [P, S], F32, tag="slot01")
-            return tile("h%d" % k, [P, S], F32, tag="h%d" % ((k + 1) % 2))
-
-        def product(k, j0):
+        def first_product(k, j0):
             g, t = divmod(k, PACK)
             acc = psum.tile([P, BANK], F32, name="acc", tag="bank")
             for a in range(K_PASSES):
@@ -194,111 +194,126 @@ def tile_list_elevator_fleet_archive_kernel(
                     lhsT=w1_w[g, a][:, t * P : (t + 1) * P].bitcast(FP8X4),
                     lhsT_scale=w1_s[g, a][:, t * P : (t + 1) * P],
                     rhs=got_w[a][:, j0 : j0 + BANK].bitcast(FP8X4),
-                    rhs_scale=got_s[4 * a : P, j0 : j0 + BANK],
+                    rhs_scale=got_s[SCALE_ROWS * a : P, j0 : j0 + BANK],
                     start=(a == 0),
                     stop=(a == K_PASSES - 1),
                 )
             return acc
 
-        def first_product(k):
-            if k in sums:
-                clipped[k] = clipped_tile(k)
-                clip(k, clipped[k][:], sums[k])
-                return
-            clipped[k] = clipped_tile(k)
-            for j0 in range(0, S, BANK):
-                clip(k, clipped[k][:, j0 : j0 + BANK], product(k, j0)[:])
+        def clip(k, out, in0):
+            g, t = divmod(k, PACK)
+            nc.vector.tensor_scalar(
+                out=out, in0=in0, scalar1=lo_t[:, g, t : t + 1], scalar2=hi_t[:, g, t : t + 1],
+                op0=ALU.max, op1=ALU.min,
+            )
 
-        sums = {}
         first = []
-        for i, j0 in enumerate(range(0, S, BANK)):
+        for i in range(S // BANK):
             first.append(tile("h_first%d" % i, [P, BANK], F32, tag="h%d" % i))
-            clip(0, first[i][:], product(0, j0)[:])
+            clip(0, first[i][:], first_product(0, i * BANK)[:])
+
+        sums, clipped = {}, {}
 
         def copy_sums(k, held):
             sums[k] = held
             for j0 in range(0, S, BANK):
-                nc.scalar.copy(out=sums[k][:, j0 : j0 + BANK], in_=product(k, j0)[:])
+                nc.scalar.copy(out=held[:, j0 : j0 + BANK], in_=first_product(k, j0)[:])
 
-        for k, tag in ((1, "sums1"), (2, "slot00"), (3, "slot01")):
+        for k, tag in ((1, "sums"), (2, "w1_00"), (3, "w1_01")):
             copy_sums(k, tile("sums%d" % k, [P, S], F32, tag=tag)[:])
 
-        damping(0)
-        damping(1)
-        quantize_w1(1, 0, 0, (0, PASS))
-        damping(2)
-        quantize_w1(1, 1, 0, (0, P, 2 * P, PASS))
-        damping(3)
+        begin_factor(0, LEAD)
+        begin_factor(1)
+        quantize_w1(1, 0, nc.scalar.copy)
+        quantize_w1(1, 1, nc.scalar.copy)
 
-        def scatter_first(i):
-            places = idx2[:, i * BANK // 16 : (i + 1) * BANK // 16]
-            nc.vector.tensor_tensor(
-                page[0][:].indirect(places), first[i][:], wgs_t[0][:, i * BANK : (i + 1) * BANK], ALU.mult
-            )
-
-        def scatter(k):
-            if k == 0:
-                scatter_first(1)
+        def clip_plane(k):
+            if k == PLANES - 1:
+                tag = "w1_01"
             else:
-                nc.vector.tensor_tensor(page[k][:].indirect(idx2[:]), clipped[k][:], wgs_t[k % PACK][:], ALU.mult)
+                tag = "h%d" % ((k + 1 if k < PACK else k) % 2)
+            clipped[k] = tile("h%d" % k, [P, S], F32, tag=tag)
+            clip(k, clipped[k][:], sums[k])
+
+        def scatter(k, h, j0, j1):
+            places = idx2[:, j0 // STRIPE : j1 // STRIPE]
+            nc.vector.tensor_tensor(page[k][:].indirect(places), h, wgs_t[k % PACK][:, j0:j1], ALU.mult)
+
+        def store_plane(k):
             nc.sync.dma_start(out=out1_rows[k // PACK, k % PACK], in_=page[k][:])
 
         page_w = [tile("page_w%d" % g, [P, T2], I32) for g in range(GROUPS)]
         page_s = [tile("page_s%d" % g, [P, T2], U8) for g in range(GROUPS)]
-        pairs = {}
+        pairs, woven_pair = {}, {}
 
         def round_plane(k, c):
             g, t = divmod(k, PACK)
             if t == 0:
                 pairs[g, c] = tile("pairs%d%d" % (g, c), [P, 2, BANK, 2], BF16, tag=pair_tags[c])
-            nc.scalar.copy(out=pairs[g, c][:, t // 2, :, t % 2], in_=page[k][:, c * BANK : (c + 1) * BANK])
+            nc.scalar.copy(out=pairs[g, c][:, t // 2, :, t % 2], in_=page[k][:, chunk[c]])
 
         def quantize_chunk(g, c):
-            cols = slice(c * BANK, (c + 1) * BANK)
-            woven = tile("woven%d%d" % (g, c), [P, BANK * PACK], BF16, tag="slot0%d" % (c % 2))
-            copy = nc.vector.tensor_copy if g == GROUPS - 1 and c < 2 else nc.scalar.copy
+            width = BANK * PACK
+            if c % 2 == 0:
+                woven_pair[g] = tile("woven%d%d" % (g, c), [P, 2 * width], BF16, tag="w1_0%d" % (c // 2))
+            woven = woven_pair[g][:, (c % 2) * width : (c % 2 + 1) * width]
+            copy = nc.vector.tensor_copy if (g, c) in WOVEN_BY_VECTOR else nc.scalar.copy
             copy(
-                out=woven[:].bitcast(F32).rearrange("p (m u) -> p m u", u=2),
+                out=woven.bitcast(F32).rearrange("p (m u) -> p m u", u=2),
                 in_=pairs[g, c][:].rearrange("p u m e -> p u (m e)").bitcast(F32).rearrange("p u m -> p m u"),
             )
-            nc.vector.quantize_mx(out=page_w[g][:, cols].bitcast(FP8X4), scales=page_s[g][:, cols], in_=woven[:])
-
-        def store_words(g, c0, c1):
-            nc.sync.dma_start(
-                out=out_2[g].rearrange("p m t -> p (m t)").bitcast(I32)[:, c0:c1], in_=page_w[g][:, c0:c1]
+            nc.vector.quantize_mx(
+                out=page_w[g][:, chunk[c]].bitcast(FP8X4), scales=page_s[g][:, chunk[c]], in_=woven
             )
 
-        def store_scales(g, queue):
+        def store_words(g, cols):
+            words = out_2[g].rearrange("p m t -> p (m t)").bitcast(I32)
+            nc.sync.dma_start(out=words[:, cols], in_=page_w[g][:, cols])
+
+        def store_scales(g):
             for q in range(QUADS):
-                queue.dma_start(
-                    out=out_3[g, 4 * q : 4 * q + 4, :].bitcast(I32),
-                    in_=page_s[g][32 * q : 32 * q + 4, :].bitcast(I32),
+                nc.sync.dma_start(
+                    out=out_3[g, SCALE_ROWS * q : SCALE_ROWS * (q + 1), :].bitcast(I32),
+                    in_=page_s[g][QUAD * q : QUAD * q + SCALE_ROWS, :].bitcast(I32),
                 )
 
-        scatter_first(0)
-        for k in range(PLANES):
-            if k + 1 < PLANES:
-                first_product(k + 1)
-            scatter(k)
-            if k == PACK - 1:
-                copy_sums(5, tile("sums5", [P, S], F32, tag="sums1")[:])
-                last_two = tile("sums67", [P, 2, S], F32, tag="slot10")
-                copy_sums(6, last_two[:, 0, :])
-                copy_sums(7, last_two[:, 1, :])
-                for plane in range(PACK):
-                    for c in range(CHUNKS):
-                        round_plane(plane, c)
-                for c in range(CHUNKS):
-                    quantize_chunk(0, c)
-            if k == PLANES - 2:
-                store_words(0, 0, T2)
-                store_scales(0, nc.sync)
-        for plane in range(PACK, PLANES - 1):
+        scatter(0, first[0][:], 0, BANK)
+        clip_plane(1)
+        scatter(0, first[1][:], BANK, S)
+        store_plane(0)
+        for k in range(1, PACK - 1):
+            clip_plane(k + 1)
+            scatter(k, clipped[k][:], 0, S)
+            store_plane(k)
+        copy_sums(4, tile("sums4", [P, S], F32, tag="h1")[:])
+        copy_sums(5, tile("sums5", [P, S], F32, tag="sums")[:])
+        last_two = tile("sums67", [P, 2, S], F32, tag="w1_10")
+        copy_sums(6, last_two[:, 0, :])
+        copy_sums(7, last_two[:, 1, :])
+        begin_factor(2)
+        begin_factor(3)
+        clip_plane(PACK)
+        scatter(PACK - 1, clipped[PACK - 1][:], 0, S)
+        store_plane(PACK - 1)
+        for k in range(PACK):
             for c in range(CHUNKS):
-                round_plane(plane, c)
+                round_plane(k, c)
+        for c in range(CHUNKS):
+            quantize_chunk(0, c)
 
-        def second_product(c, factor):
-            cols = slice(c * BANK, (c + 1) * BANK)
+        for k in range(PACK, PLANES - 1):
+            clip_plane(k + 1)
+            scatter(k, clipped[k][:], 0, S)
+            store_plane(k)
+        store_words(0, slice(0, T2))
+        store_scales(0)
+        scatter(PLANES - 1, clipped[PLANES - 1][:], 0, S)
+        store_plane(PLANES - 1)
+        for k in range(PACK, PLANES - 1):
+            for c in range(CHUNKS):
+                round_plane(k, c)
+
+        def second_product(c, factor, per_store):
             for b in range(N_TILES):
                 acc = psum.tile([P, BANK], F32, name="acc", tag="bank")
                 for g in range(GROUPS):
@@ -306,22 +321,29 @@ def tile_list_elevator_fleet_archive_kernel(
                         out=acc[:],
                         lhsT=w2_w[:, g, 2 * b * P : 2 * (b + 1) * P].bitcast(FP4X4),
                         lhsT_scale=w2_s[:, g, b * P : (b + 1) * P],
-                        rhs=page_w[g][:, cols].bitcast(FP8X4),
-                        rhs_scale=page_s[g][:, cols],
+                        rhs=page_w[g][:, chunk[c]].bitcast(FP8X4),
+                        rhs_scale=page_s[g][:, chunk[c]],
                         start=(g == 0),
                         stop=(g == GROUPS - 1),
                     )
                 nc.vector.tensor_tensor(factor[:, b, :], acc[:], factor[:, b, :], ALU.mult)
-                if b % 2 == 1:
-                    nc.sync.dma_start(out=out0_rows[:, b - 1 : b + 1, cols], in_=factor[:, b - 1 : b + 1, :])
+                if (b + 1) % per_store == 0:
+                    rows = slice(b + 1 - per_store, b + 1)
+                    nc.sync.dma_start(out=out0_rows[:, rows, chunk[c]], in_=factor[:, rows, :])
 
         for c in range(CHUNKS):
             round_plane(PLANES - 1, c)
             quantize_chunk(1, c)
-            store_words(1, c * BANK, (c + 1) * BANK)
-            if c > 0:
-                second_product(c - 1, damp[:, :, (c - 1) * BANK : c * BANK])
-        damp_last = tile("damp_last", [P, N_TILES, BANK], F32, tag="slot11")
-        nc.scalar.activation(out=damp_last[:], in_=damp[:, :, last], func=ACT.Square)
-        store_scales(1, nc.sync)
-        second_product(CHUNKS - 1, damp_last[:])
+            store_words(1, chunk[c])
+            if c in (1, 2):
+                second_product(c - 1, damp[:, :, chunk[c - 1]], per_store=2)
+        factor2 = tile("factor2", [P, N_TILES, BANK], F32, tag="w1_11")
+        factor3 = tile("factor3", [P, N_TILES, BANK], F32, tag="w1_00")
+        square(factor2[:], damp[:, :, chunk[2]])
+        for b0 in range(0, N_TILES, 2):
+            root(factor3[:, b0 : b0 + 2, :], damp[:, b0 : b0 + 2, chunk[3]])
+        for b0 in range(0, N_TILES, 2):
+            square(factor3[:, b0 : b0 + 2, :], factor3[:, b0 : b0 + 2, :])
+        second_product(2, factor2[:], per_store=2)
+        store_scales(1)
+        second_product(3, factor3[:], per_store=1)

from contextlib import ExitStack

import concourse.mybir as mybir

K, H, N, T, S, T2 = 1024, 1024, 512, 2048, 1024, 2048
FLOPS = 2 * K * H * S + 2 * H * N * T2

F32 = mybir.dt.float32
BF16 = mybir.dt.bfloat16
I32 = mybir.dt.int32
U32 = mybir.dt.uint32
U16 = mybir.dt.uint16
U8 = mybir.dt.uint8
FP8X4 = mybir.dt.float8_e4m3fn_x4
FP4X4 = mybir.dt.float4_e2m1fn_x4
ALU = mybir.AluOpType
ACT = mybir.ActivationFunctionType

P = 128
PACK = 4
PASS = P * PACK
QUADS = 4
QUAD = P // QUADS
SCALE_ROWS = 4
STRIPE = 16
BANK = 512
BANKS = 8
K_PASSES = K // PASS
GROUPS = H // PASS
PLANES = GROUPS * PACK
CHUNKS = T2 // BANK
N_TILES = N // P
LEAD = 64
WOVEN_BY_VECTOR = ((0, 2), (0, 3), (1, 0), (1, 1))


def tile_list_elevator_fleet_archive_kernel(
    tc, tab_words, tab_scales, offs, offs2, w1, lo, hi, wgs, page0, w2_words, w2_scales, load,
    out_0, out_1, out_2, out_3,
):
    nc = tc.nc
    with ExitStack() as ctx:
        lists = ctx.enter_context(tc.tile_pool(name="lists", bufs=1))
        sb = ctx.enter_context(tc.tile_pool(name="sb", bufs=1))
        psum = ctx.enter_context(tc.psum_pool(name="psum", bufs=BANKS))

        def tile(name, shape, dtype, tag=None):
            return sb.tile(shape, dtype, name=name, tag=tag or name, bufs=1, align_bytes=64)

        idx = lists.tile([P, S // STRIPE], U16, name="idx")
        idx2 = lists.tile([P, S // STRIPE], U16, name="idx2")
        tab_w = [tile("tab_w%d" % a, [P, T], I32) for a in range(K_PASSES)]
        tab_s = tile("tab_s", [P, T], U8)
        w1_raw = {
            (g, a): tile("w1_raw%d%d" % (g, a), [P, PACK, PASS], F32, tag="w1_%d%d" % (g, a))
            for g in range(GROUPS) for a in range(K_PASSES)
        }
        lo_t = tile("lo_t", [P, GROUPS, PACK], F32)
        hi_t = tile("hi_t", [P, GROUPS, PACK], F32)
        wgs_t = [tile("wgs%d" % t, [P, S], F32) for t in range(PACK)]
        page = [tile("page%d" % k, [P, T2], F32) for k in range(PLANES)]
        damp = tile("damp", [P, N_TILES, T2], F32)
        w2_w = tile("w2_w", [P, GROUPS, 2 * N], U8)
        w2_s = tile("w2_s", [P, GROUPS, N], U8)

        w1_rows = w1.rearrange("(a p i) r -> a p i r", a=K_PASSES, i=PACK)
        wgs_rows = wgs.rearrange("(q t) j -> t q j", t=PACK)
        page_rows = page0.rearrange("(g p t) m -> g t p m", g=GROUPS, t=PACK)
        out1_rows = out_1.rearrange("(g p t) m -> g t p m", g=GROUPS, t=PACK)
        load_rows = load.rearrange("(b p) m -> p b m", p=P)
        out0_rows = out_0.rearrange("(b p) m -> p b m", p=P)

        def load_w1(g, a):
            nc.sync.dma_start(out=w1_raw[g, a][:], in_=w1_rows[a, :, :, g * PASS : (g + 1) * PASS])

        def load_table(a):
            nc.sync.dma_start(out=tab_w[a][:], in_=tab_words[a].rearrange("p t i -> p (t i)").bitcast(I32))

        def load_wgs(t, j0=0, j1=S):
            for q in (0, 2, 1, 3):
                nc.sync.dma_start(out=wgs_t[t][QUAD * q : QUAD * (q + 1), j0:j1], in_=wgs_rows[t, :, j0:j1])

        def load_page(k):
            nc.sync.dma_start(out=page[k][:], in_=page_rows[k // PACK, k % PACK])

        def load_load(b, m0=0):
            nc.sync.dma_start(out=damp[:, b, m0:], in_=load_rows[:, b, m0:])

        nc.vector.memset(tab_s[:].bitcast(I32), 0)
        nc.vector.memset(w2_s[:].bitcast(I32), 0)
        for q in range(QUADS):
            nc.scalar.dma_start(
                out=tab_s[QUAD * q : QUAD * q + SCALE_ROWS * K_PASSES, :].bitcast(I32),
                in_=tab_scales[:, SCALE_ROWS * q : SCALE_ROWS * (q + 1), :].bitcast(I32),
            )
        nc.scalar.dma_start(out=damp[:, 0, :LEAD], in_=load_rows[:, 0, :LEAD])
        nc.scalar.dma_start(out=lo_t[:], in_=lo.rearrange("(g p t) -> p g t", g=GROUPS, t=PACK))
        nc.scalar.dma_start(out=hi_t[:], in_=hi.rearrange("(g p t) -> p g t", g=GROUPS, t=PACK))

        nc.sync.dma_start(idx[:], offs)
        load_table(0)
        load_w1(0, 0)
        load_w1(0, 1)
        load_table(1)
        nc.sync.dma_start(idx2[:], offs2)
        load_wgs(0, 0, BANK)
        load_page(0)
        load_wgs(0, BANK, S)
        load_load(0, LEAD)
        load_page(1)
        load_wgs(1)
        load_load(1)
        load_page(2)
        load_wgs(2)
        load_w1(1, 0)
        load_w1(1, 1)
        load_load(2)
        load_page(3)
        load_wgs(3)
        load_load(3)
        for k in range(PACK, PLANES):
            load_page(k)
        nc.sync.dma_start(out=w2_w[:].bitcast(I32), in_=w2_words.rearrange("g p c -> p g c").bitcast(I32))
        for q in range(QUADS):
            nc.sync.dma_start(
                out=w2_s[QUAD * q : QUAD * q + SCALE_ROWS, :, :].bitcast(I32),
                in_=w2_scales[:, SCALE_ROWS * q : SCALE_ROWS * (q + 1), :].rearrange("g r c -> r g c").bitcast(I32),
            )

        got_s = tile("got_s", [P, S], U8)
        got_w = [tile("got_w%d" % a, [P, S], I32) for a in range(K_PASSES)]

        def gather_words(a, j0, j1):
            window = tab_w[a][:].bitcast(U32)
            entries = idx[:, j0 // STRIPE : j1 // STRIPE]
            nc.vector.tensor_copy(got_w[a][:, j0:j1].bitcast(U32), window.indirect(entries))

        w1_w, w1_s = {}, {}

        def quantize_w1(g, a, copy):
            dealt = tile("w1_bf%d%d" % (g, a), [P, PACK, P, PACK], BF16, tag="w1_bf%d" % a)
            copy(
                out=dealt[:].rearrange("p t m i -> p m t i"),
                in_=w1_raw[g, a][:].rearrange("p i (m t) -> p m t i", t=PACK),
            )
            w1_w[g, a] = tile("w1_w%d%d" % (g, a), [P, PASS], I32)
            w1_s[g, a] = tile("w1_s%d%d" % (g, a), [P, PASS], U8)
            nc.vector.quantize_mx(
                out=w1_w[g, a][:].bitcast(FP8X4),
                scales=w1_s[g, a][:],
                in_=dealt[:].rearrange("p t m i -> p (t m i)"),
            )

        chunk = [slice(c * BANK, (c + 1) * BANK) for c in range(CHUNKS)]
        pair_tags = ("w1_11", "work0", "work1", "work2")

        def magnitude(out, in_):
            nc.scalar.activation(out=out, in_=in_, func=ACT.Abs)

        def root(out, in_):
            nc.scalar.activation(out=out, in_=in_, func=ACT.Abs_reciprocal_sqrt, bias=1.0)

        def square(out, in_):
            nc.scalar.activation(out=out, in_=in_, func=ACT.Square)

        def begin_factor(b, m0=0):
            work = [tile("work%d%d" % (b, c), [P, BANK], F32, tag=pair_tags[c + 1]) for c in range(CHUNKS - 1)]
            row = damp[:, b, :]
            magnitude(row[:, m0 : 2 * BANK], row[:, m0 : 2 * BANK])
            magnitude(work[2][:], row[:, chunk[2]])
            magnitude(row[:, chunk[3]], row[:, chunk[3]])
            root(work[0][:, m0:], row[:, m0:BANK])
            root(work[1][:], row[:, chunk[1]])
            root(row[:, chunk[2]], work[2][:])
            square(row[:, m0:BANK], work[0][:, m0:])
            square(row[:, chunk[1]], work[1][:])

        for step in (magnitude, root, square):
            step(damp[:, 0, :LEAD], damp[:, 0, :LEAD])

        nc.vector.tensor_copy(got_s[:], tab_s[:].indirect(idx[:]))
        gather_words(0, 0, S)
        quantize_w1(0, 0, nc.scalar.copy)
        quantize_w1(0, 1, nc.vector.tensor_copy)
        gather_words(1, 0, BANK)
        gather_words(1, BANK, S)

        def first_product(k, j0):
            g, t = divmod(k, PACK)
            acc = psum.tile([P, BANK], F32, name="acc", tag="bank")
            for a in range(K_PASSES):
                nc.tensor.matmul_mx(
                    out=acc[:],
                    lhsT=w1_w[g, a][:, t * P : (t + 1) * P].bitcast(FP8X4),
                    lhsT_scale=w1_s[g, a][:, t * P : (t + 1) * P],
                    rhs=got_w[a][:, j0 : j0 + BANK].bitcast(FP8X4),
                    rhs_scale=got_s[SCALE_ROWS * a : P, j0 : j0 + BANK],
                    start=(a == 0),
                    stop=(a == K_PASSES - 1),
                )
            return acc

        def clip(k, out, in0):
            g, t = divmod(k, PACK)
            nc.vector.tensor_scalar(
                out=out, in0=in0, scalar1=lo_t[:, g, t : t + 1], scalar2=hi_t[:, g, t : t + 1],
                op0=ALU.max, op1=ALU.min,
            )

        first = []
        for i in range(S // BANK):
            first.append(tile("h_first%d" % i, [P, BANK], F32, tag="h%d" % i))
            clip(0, first[i][:], first_product(0, i * BANK)[:])

        sums, clipped = {}, {}

        def copy_sums(k, held):
            sums[k] = held
            for j0 in range(0, S, BANK):
                nc.scalar.copy(out=held[:, j0 : j0 + BANK], in_=first_product(k, j0)[:])

        for k, tag in ((1, "sums"), (2, "w1_00"), (3, "w1_01")):
            copy_sums(k, tile("sums%d" % k, [P, S], F32, tag=tag)[:])

        begin_factor(0, LEAD)
        begin_factor(1)
        quantize_w1(1, 0, nc.scalar.copy)
        quantize_w1(1, 1, nc.scalar.copy)

        def clip_plane(k):
            if k == PLANES - 1:
                tag = "w1_01"
            else:
                tag = "h%d" % ((k + 1 if k < PACK else k) % 2)
            clipped[k] = tile("h%d" % k, [P, S], F32, tag=tag)
            clip(k, clipped[k][:], sums[k])

        def scatter(k, h, j0, j1):
            places = idx2[:, j0 // STRIPE : j1 // STRIPE]
            nc.vector.tensor_tensor(page[k][:].indirect(places), h, wgs_t[k % PACK][:, j0:j1], ALU.mult)

        def store_plane(k):
            nc.sync.dma_start(out=out1_rows[k // PACK, k % PACK], in_=page[k][:])

        page_w = [tile("page_w%d" % g, [P, T2], I32) for g in range(GROUPS)]
        page_s = [tile("page_s%d" % g, [P, T2], U8) for g in range(GROUPS)]
        pairs, woven_pair = {}, {}

        def round_plane(k, c):
            g, t = divmod(k, PACK)
            if t == 0:
                pairs[g, c] = tile("pairs%d%d" % (g, c), [P, 2, BANK, 2], BF16, tag=pair_tags[c])
            nc.scalar.copy(out=pairs[g, c][:, t // 2, :, t % 2], in_=page[k][:, chunk[c]])

        def quantize_chunk(g, c):
            width = BANK * PACK
            if c % 2 == 0:
                woven_pair[g] = tile("woven%d%d" % (g, c), [P, 2 * width], BF16, tag="w1_0%d" % (c // 2))
            woven = woven_pair[g][:, (c % 2) * width : (c % 2 + 1) * width]
            copy = nc.vector.tensor_copy if (g, c) in WOVEN_BY_VECTOR else nc.scalar.copy
            copy(
                out=woven.bitcast(F32).rearrange("p (m u) -> p m u", u=2),
                in_=pairs[g, c][:].rearrange("p u m e -> p u (m e)").bitcast(F32).rearrange("p u m -> p m u"),
            )
            nc.vector.quantize_mx(
                out=page_w[g][:, chunk[c]].bitcast(FP8X4), scales=page_s[g][:, chunk[c]], in_=woven
            )

        def store_words(g, cols):
            words = out_2[g].rearrange("p m t -> p (m t)").bitcast(I32)
            nc.sync.dma_start(out=words[:, cols], in_=page_w[g][:, cols])

        def store_scales(g):
            for q in range(QUADS):
                nc.sync.dma_start(
                    out=out_3[g, SCALE_ROWS * q : SCALE_ROWS * (q + 1), :].bitcast(I32),
                    in_=page_s[g][QUAD * q : QUAD * q + SCALE_ROWS, :].bitcast(I32),
                )

        scatter(0, first[0][:], 0, BANK)
        clip_plane(1)
        scatter(0, first[1][:], BANK, S)
        store_plane(0)
        for k in range(1, PACK - 1):
            clip_plane(k + 1)
            scatter(k, clipped[k][:], 0, S)
            store_plane(k)
        copy_sums(4, tile("sums4", [P, S], F32, tag="h1")[:])
        copy_sums(5, tile("sums5", [P, S], F32, tag="sums")[:])
        last_two = tile("sums67", [P, 2, S], F32, tag="w1_10")
        copy_sums(6, last_two[:, 0, :])
        copy_sums(7, last_two[:, 1, :])
        begin_factor(2)
        begin_factor(3)
        clip_plane(PACK)
        scatter(PACK - 1, clipped[PACK - 1][:], 0, S)
        store_plane(PACK - 1)
        for k in range(PACK):
            for c in range(CHUNKS):
                round_plane(k, c)
        for c in range(CHUNKS):
            quantize_chunk(0, c)

        for k in range(PACK, PLANES - 1):
            clip_plane(k + 1)
            scatter(k, clipped[k][:], 0, S)
            store_plane(k)
        store_words(0, slice(0, T2))
        store_scales(0)
        scatter(PLANES - 1, clipped[PLANES - 1][:], 0, S)
        store_plane(PLANES - 1)
        for k in range(PACK, PLANES - 1):
            for c in range(CHUNKS):
                round_plane(k, c)

        def second_product(c, factor, per_store):
            for b in range(N_TILES):
                acc = psum.tile([P, BANK], F32, name="acc", tag="bank")
                for g in range(GROUPS):
                    nc.tensor.matmul_mx(
                        out=acc[:],
                        lhsT=w2_w[:, g, 2 * b * P : 2 * (b + 1) * P].bitcast(FP4X4),
                        lhsT_scale=w2_s[:, g, b * P : (b + 1) * P],
                        rhs=page_w[g][:, chunk[c]].bitcast(FP8X4),
                        rhs_scale=page_s[g][:, chunk[c]],
                        start=(g == 0),
                        stop=(g == GROUPS - 1),
                    )
                nc.vector.tensor_tensor(factor[:, b, :], acc[:], factor[:, b, :], ALU.mult)
                if (b + 1) % per_store == 0:
                    rows = slice(b + 1 - per_store, b + 1)
                    nc.sync.dma_start(out=out0_rows[:, rows, chunk[c]], in_=factor[:, rows, :])

        for c in range(CHUNKS):
            round_plane(PLANES - 1, c)
            quantize_chunk(1, c)
            store_words(1, chunk[c])
            if c in (1, 2):
                second_product(c - 1, damp[:, :, chunk[c - 1]], per_store=2)
        factor2 = tile("factor2", [P, N_TILES, BANK], F32, tag="w1_11")
        factor3 = tile("factor3", [P, N_TILES, BANK], F32, tag="w1_00")
        square(factor2[:], damp[:, :, chunk[2]])
        for b0 in range(0, N_TILES, 2):
            root(factor3[:, b0 : b0 + 2, :], damp[:, b0 : b0 + 2, chunk[3]])
        for b0 in range(0, N_TILES, 2):
            square(factor3[:, b0 : b0 + 2, :], factor3[:, b0 : b0 + 2, :])
        second_product(2, factor2[:], per_store=2)
        store_scales(1)
        second_product(3, factor3[:], per_store=1)
